import numpy as np
CORES = [8,136,40,168]
N = 4
R, L = 4096, 1024
def entries(a): return a.T.reshape(-1)
def pack(v, P): return np.ascontiguousarray(np.asarray(v, np.int32).reshape(-1, P).T)
def lists(rng, how):
    n = N * L
    h, g = rng.integers(0, N, n), rng.permutation(np.repeat(np.arange(N), L))
    if how == "hotrank":
        a, b = rng.permutation(N)[:2]; M = min(R, n); h[:] = a
        g = np.concatenate([np.full(M, b), rng.permutation(np.repeat(np.delete(np.arange(N), [a, b]), L))[:n - M]]).reshape(N, L)[rng.permutation(N)].reshape(-1)
    if how == "third":
        a, b = 1 + rng.permutation(N - 1)[:2]; h, g = (np.arange(n) // L + a) % N, (np.arange(n) // L + b) % N
    d = np.zeros(n, np.int64)
    for q in range(N): m = np.nonzero(g == q)[0]; d[m] = R * q + np.concatenate([[0, R - 1], 1 + rng.permutation(R - 2)])[:len(m)]
    s = R * h + rng.integers(0, R, n)
    if how == "fork": s = R * h + rng.integers(0, R, N)[h]
    if how == "chain":
        for q in range(N):
            m = np.nonzero(h == q)[0]; w = d[g == q]
            s[m] = w[rng.integers(0, len(w), len(m))]
    if how == "gaps":
        z = rng.permutation(N)[:3]; k = (rng.random(n) < 0.5) | (np.arange(n) // L == z[0]) | (h == z[1]) | (g == z[2]); s[k] = -1; d[k] = -1
    return {"src": np.stack([pack(v, 16) for v in s.reshape(N, L)]), "dst": np.stack([pack(v, 16) for v in d.reshape(N, L)])}
def setup_inputs(rng):
    return dict({"tab": rng.standard_normal((N, 128, R), dtype=np.float32)}, **lists(rng, "uniform"))
def setup_inputs_chain(rng):
    d = setup_inputs(rng); d.update(lists(rng, "chain"))
    for k in ("tab",): d[k] = (d[k].astype(np.float32) * 1048576.0).astype(d[k].dtype)
    return d
def setup_inputs_fork(rng):
    d = setup_inputs(rng); d.update(lists(rng, "fork"))
    for k in ("tab",): d[k] = (d[k].astype(np.float32) * (1 / 1024.0)).astype(d[k].dtype)
    return d
def setup_inputs_gaps(rng):
    d = setup_inputs(rng); d.update(lists(rng, "gaps"))
    return d
def setup_inputs_hotrank(rng):
    d = setup_inputs(rng); d.update(lists(rng, "hotrank"))
    return d
def setup_inputs_third(rng):
    d = setup_inputs(rng); d.update(lists(rng, "third"))
    return d
def check_inputs(x):
    bad = []; s, d = x["src"].reshape(-1), x["dst"].reshape(-1); k = d >= 0
    if s.min() < -1 or s.max() >= N * R or d.min() < -1 or d.max() >= N * R: bad.append("out of range")
    if ((s < 0) != (d < 0)).any(): bad.append("half a pair")
    if len(np.unique(d[k])) != int(k.sum()): bad.append("a column is written twice")
    return bad
def reference(tab, src, dst):
    A = np.concatenate(list(tab), axis=1); Y = A.copy()
    for r in range(N):
        s, d = entries(src[r]), entries(dst[r]); k = d >= 0
        Y[:, d[k]] = A[:, s[k]]
    return {"y": np.stack([Y[:, R * r:R * r + R] for r in range(N)])}

@@ -1,0 +1,291 @@
+from concourse.bass import DstId, RemoteDMATransfer
+from concourse.mybir import AluOpType, ActivationFunctionType
+
+N, R, L = 4, 4096, 1024
+K = 4
+S = L // K
+HELPERS = 2
+SW, DW = L // 16, L // 128
+TW = SW + DW
+YB = 512
+NY = R // YB
+
+SCRATCH = {
+    "F": ("sbuf", [128, N * L + R], "float32"),
+    "G": ("sbuf", [128, N * L], "float32"),
+    "Y": ("sbuf", [128, R], "float32"),
+    "H": ("sbuf", [128, (K // HELPERS) * N * S], "float32"),
+    "M": ("sbuf", [128, (K // HELPERS) * S], "float32"),
+    "LS": ("sbuf", [128, N * TW], "int32"),
+    "O1": ("sbuf", [128, N * SW], "uint16"),
+    "O2": ("sbuf", [128, (K // HELPERS) * (S // 16)], "uint16"),
+    "O3": ("sbuf", [128, R // 16], "uint16"),
+    "DS": ("sbuf", [128, N * DW], "int32"),
+    "KI": ("sbuf", [128, N * DW], "int32"),
+    "BI": ("sbuf", [128, N * DW], "int32"),
+    "KD": ("sbuf", [128, N * DW], "float32"),
+    "BD": ("sbuf", [128, N * DW], "float32"),
+    "W": ("sbuf", [128, N * DW], "float32"),
+    "iw": ("sbuf", [128, N * DW], "int32"),
+    "ip": ("sbuf", [128, 1], "int32"),
+    "q15": ("sbuf", [128, 1], "int32"),
+    "q7": ("sbuf", [128, 1], "int32"),
+    "q3": ("sbuf", [128, 1], "int32"),
+    "f15": ("sbuf", [128, 1], "float32"),
+    "f7": ("sbuf", [128, 1], "float32"),
+    "f3": ("sbuf", [128, 1], "float32"),
+    "ib": ("sbuf", [128, R // 16], "bfloat16"),
+    "ia": ("sbuf", [128, 128], "bfloat16"),
+    "ic": ("sbuf", [128, R // 16], "int32"),
+    "C": ("sbuf", [128, R // 16], "float32"),
+    "A": ("sbuf", [128, N * DW * 128], "float16"),
+    "B": ("sbuf", [128, N * DW * (R // 16)], "float16"),
+    "t1": ("sbuf", [128, R // 16], "float32"),
+    "t2": ("sbuf", [128, R // 16], "float32"),
+    "t3": ("sbuf", [128, R // 16], "float32"),
+    "t4": ("sbuf", [128, R // 16], "float32"),
+    "t5": ("sbuf", [128, R // 16], "float32"),
+    "ti": ("sbuf", [128, 64], "int32"),
+    "ps": ("psum", [128, R // 16], "float32"),
+}
+SEMAPHORES = (["ld", "gate", "tl", "ls", "o1", "lo", "o2", "f2", "gi", "vs", "mm", "o3", "st"]
+              + ["ga%d" % k for k in range(K)] + ["h1_%d" % k for k in range(K)] + ["mg%d" % k for k in range(K)]
+              + ["oh%d" % r for r in range(N)] + ["fy%d" % j for j in range(NY)])
+
+
+def bits(m):
+    return [1 << e for e in range(16) if (m >> e) & 1]
+
+
+def rank_program(g, core, T, topo):
+    op = AluOpType
+    V = g.vector
+
+    def helpers(rc):
+        c = [x for x in range(256) if topo.host(x) == topo.host(rc) and topo.chip(x) == topo.chip(rc)
+             and topo.die(x) != topo.die(rc)]
+        return c[:HELPERS]
+
+    def dest(dst):
+        rid, pid = topo.addr(dst, core)
+        return DstId(rid=rid, pnc=pid)
+
+    def engines(src):
+        mine = [c for c in T.cores if topo.host(c) == topo.host(src) and topo.chip(c) == topo.chip(src)][0]
+        far = [c for c in T.cores if c != mine][0]
+        near = [c for c in helpers(mine) + [mine] if c != src][0]
+        off = topo.mask(src, far)
+        return bits(off), bits(topo.mask(src, near) & ~off)
+
+    def first_hop(h, k):
+        off, on = engines(T.cores[h])
+        rem = [(h + d) % N for d in range(1, N)]
+        n = len(off)
+        if k % 2 == 0:
+            cut = [off[:n // 2], off[n // 2:3 * n // 4], off[3 * n // 4:]]
+        else:
+            cut = [off[:n // 4], off[n // 4:n // 2], off[n // 2:]]
+        m = {rem[i]: cut[i] for i in range(N - 1)}
+        m[h] = on
+        return m
+
+    cnt = [0]
+
+    def v(ins):
+        ins.then_inc(T.sem.vs, 1)
+        cnt[0] += 1
+
+    def vw():
+        V.wait_ge(T.sem.vs, cnt[0])
+
+    q = T.rank_of(core)
+    if q is None:
+        own = [r for r in range(N) if core in helpers(T.cores[r])]
+        if own:
+            helper_program(g, core, T, own[0], helpers(T.cores[own[0]]).index(core), dest, engines, first_hop, v, vw)
+        return
+
+    off, on = engines(core)
+    others = [c for c in T.cores if c != core]
+    mine = helpers(core)
+    b = TW * q
+    for a in range(8):
+        e = g.sync if a % 2 == 0 else g.scalar
+        e.dma_start(T.LS[16 * a:16 * a + 16, b:b + SW], T.src[:]).then_inc(T.sem.ld, 16)
+    g.scalar.dma_start(T.LS[:, b + SW:b + TW], T.dst[:]).then_inc(T.sem.ld, 16)
+    half = R // 2
+    g.sync.dma_start(T.F[:, N * L:N * L + half], T.tab[:, 0:half]).then_inc(T.sem.tl, 16)
+    g.sync.wait_ge(T.sem.gate, 1)
+    g.sync.dma_start(T.F[:, N * L + half:N * L + R], T.tab[:, half:R]).then_inc(T.sem.tl, 16)
+    tile = T.LS[:, b:b + TW]
+    g.wait_ge(T.sem.ld, 144)
+    g.remote_dma_fused([RemoteDMATransfer(dst_ids=[dest(c) for c in others], dma_engine_mask=sum(off),
+                                          remote_sem=T.sem.ls, srcs=[tile], dsts=[tile for c in others])],
+                       local_sem=T.sem.lo)
+    g.sem_inc(T.sem.gate, 1)
+    g.remote_dma_fused([RemoteDMATransfer(dst_ids=[dest(c) for c in mine], dma_engine_mask=sum(on),
+                                          remote_sem=T.sem.ls, srcs=[tile], dsts=[tile for c in mine])],
+                       local_sem=T.sem.lo)
+    sent = len(off) + len(on)
+    g.iota(T.ip[:], [[0, 1]], 0, 1).then_inc(T.sem.gi, 1)
+    g.iota(T.ia[:], [[0, 8], [1, 16]], 0, 0, allow_small_or_imprecise_dtypes=True).then_inc(T.sem.gi, 1)
+    g.iota(T.ib[:], [[1, R // 16]], 0, 0, allow_small_or_imprecise_dtypes=True).then_inc(T.sem.gi, 1)
+    g.iota(T.ic[:], [[16, R // 16]], 0, 0).then_inc(T.sem.gi, 1)
+    hw = N * DW // 2
+    g.iota(T.iw[:, 0:hw], [[L, N // 2], [16, DW]], -2048, 0).then_inc(T.sem.gi, 1)
+    g.iota(T.iw[:, hw:2 * hw], [[L, N // 2], [16, DW]], 1, 0).then_inc(T.sem.gi, 1)
+
+    def offsets(r):
+        V.tensor_scalar(out=T.O1[:, SW * r:SW * r + SW], in0=T.LS[:, TW * r:TW * r + SW], scalar1=float(R * q),
+                        scalar2=float(R - 1), op0=op.subtract, op1=op.min).then_inc(T.sem.o1, 1)
+    V.wait_ge(T.sem.ld, 144)
+    offsets(q)
+    arrive = (N - 1) * len(off)
+    V.wait_ge(T.sem.ls, arrive)
+    for r in range(N):
+        if r != q:
+            offsets(r)
+    V.wait_ge(T.sem.o1, N)
+    V.wait_ge(T.sem.tl, 32)
+    g.scalar.wait_ge(T.sem.o1, N)
+    g.scalar.wait_ge(T.sem.tl, 32)
+    win = T.F[:, N * L:N * L + R]
+    ow = S // 16
+    for k in range(K):
+        for r in range(N):
+            idx = T.O1[:, SW * r + ow * k:SW * r + ow * k + ow]
+            out = T.G[:, (k * N + r) * S:(k * N + r + 1) * S]
+            if r < N // 2:
+                V.tensor_copy(out, win.indirect(idx)).then_inc(T.sem["ga%d" % k], 1)
+            else:
+                g.scalar.activation(out, win.indirect(idx), ActivationFunctionType.Copy).then_inc(T.sem["ga%d" % k], 1)
+    for k in range(K):
+        plan = first_hop(q, k)
+        g.wait_ge(T.sem["ga%d" % k], N)
+        n = k // HELPERS
+        tr = []
+        for d in list(range(1, N)) + [0]:
+            r = (q + d) % N
+            hc = helpers(T.cores[r])[k % HELPERS]
+            tr.append(RemoteDMATransfer(dst_ids=[dest(hc)], dma_engine_mask=sum(plan[r]), remote_sem=T.sem["h1_%d" % k],
+                                        srcs=[T.G[:, (k * N + r) * S:(k * N + r + 1) * S]],
+                                        dsts=[T.H[:, (n * N + q) * S:(n * N + q + 1) * S]]))
+            sent += len(plan[r])
+        g.remote_dma_fused(tr, local_sem=T.sem.lo)
+
+    V.wait_ge(T.sem.gi, 6)
+    v(V.tensor_scalar(out=T.q15[:], in0=T.ip[:], scalar1=15, scalar2=None, op0=op.bitwise_and))
+    v(V.tensor_scalar(out=T.q7[:], in0=T.ip[:], scalar1=7, scalar2=None, op0=op.bitwise_and))
+    v(V.tensor_scalar(out=T.q3[:], in0=T.ip[:], scalar1=3, scalar2=None, op0=op.arith_shift_right))
+    for r in range(N):
+        v(V.tensor_copy(T.DS[:, DW * r:DW * r + DW], T.LS[:, TW * r + SW:TW * r + TW]))
+    vw()
+    v(V.tensor_copy(T.f15[:], T.q15[:]))
+    v(V.tensor_scalar(out=T.f7[:], in0=T.q7[:], scalar1=128.0, scalar2=None, op0=op.mult))
+    v(V.tensor_copy(T.f3[:], T.q3[:]))
+    v(V.tensor_scalar(out=T.KI[:], in0=T.DS[:], scalar1=4, scalar2=None, op0=op.arith_shift_right))
+    v(V.tensor_scalar(out=T.BI[:], in0=T.DS[:], scalar1=15, scalar2=None, op0=op.bitwise_and))
+    vw()
+    v(V.tensor_scalar(out=T.C[:], in0=T.ic[:], scalar1=T.f15[:], scalar2=float(N * L - 2048), op0=op.add, op1=op.add))
+    v(V.tensor_scalar(out=T.W[:], in0=T.iw[:], scalar1=T.f7[:], scalar2=T.f3[:], op0=op.add, op1=op.add))
+    v(V.tensor_scalar(out=T.KD[:], in0=T.KI[:], scalar1=float(q * R // 16), scalar2=None, op0=op.subtract))
+    v(V.tensor_copy(T.BD[:], T.BI[:]))
+    vw()
+    kw = R // 16
+    for r in range(N):
+        s = T.sem["oh%d" % r]
+        for u in range(DW):
+            c = r * DW + u
+            V.tensor_scalar(out=T.A[:, 128 * c:128 * c + 128], in0=T.ia[:], scalar1=T.BD[:, c:c + 1],
+                            scalar2=T.W[:, c:c + 1], op0=op.is_equal, op1=op.mult).then_inc(s, 1)
+            V.tensor_scalar(out=T.B[:, kw * c:kw * c + kw], in0=T.ib[:], scalar1=T.KD[:, c:c + 1],
+                            scalar2=None, op0=op.is_equal).then_inc(s, 1)
+    for r in range(N):
+        g.tensor.wait_ge(T.sem["oh%d" % r], 2 * DW)
+        for u in range(DW):
+            c = r * DW + u
+            last = c == N * DW - 1
+            ins = g.tensor.matmul(T.ps[:], T.A[:, 128 * c:128 * c + 128], T.B[:, kw * c:kw * c + kw], c == 0, last)
+            if last:
+                ins.then_inc(T.sem.mm, 1)
+    V.wait_ge(T.sem.mm, 1)
+    v(V.tensor_scalar(out=T.t1[:], in0=T.ps[:], scalar1=0.0, scalar2=None, op0=op.is_equal))
+    v(V.tensor_scalar(out=T.t2[:], in0=T.ps[:], scalar1=0.0, scalar2=2047.0, op0=op.is_le, op1=op.add))
+    vw()
+    v(V.tensor_tensor(T.t3[:], T.t1[:], T.C[:], op.mult))
+    v(V.tensor_tensor(T.t4[:], T.t2[:], T.ps[:], op.add))
+    vw()
+    v(V.tensor_tensor(T.t5[:], T.t3[:], T.t4[:], op.add))
+    vw()
+    V.tensor_copy(T.O3[:], T.t5[:]).then_inc(T.sem.o3, 1)
+    land = 0
+    for r in range(N):
+        for k in range(K):
+            o2, n2 = engines(helpers(T.cores[r])[k % HELPERS])
+            land += len(n2) if r == q else len(o2)
+    for e in (V, g.scalar):
+        e.wait_ge(T.sem.o3, 1)
+        e.wait_ge(T.sem.f2, land)
+    yw = YB // 16
+    for j in range(NY):
+        src = T.F[:].indirect(T.O3[:, yw * j:yw * j + yw])
+        out = T.Y[:, YB * j:YB * j + YB]
+        s = T.sem["fy%d" % j]
+        if j % 2 == 0:
+            V.tensor_copy(out, src).then_inc(s, 1)
+        else:
+            g.scalar.activation(out, src, ActivationFunctionType.Copy).then_inc(s, 1)
+    for j in range(NY):
+        g.sync.wait_ge(T.sem["fy%d" % j], 1)
+        g.sync.dma_start(T.y[:, YB * j:YB * j + YB], T.Y[:, YB * j:YB * j + YB]).then_inc(T.sem.st, 16)
+    g.sync.wait_ge(T.sem.st, 16 * NY)
+    g.wait_ge(T.sem.lo, sent)
+
+
+def helper_program(g, core, T, r, a, dest, engines, first_hop, v, vw):
+    op = AluOpType
+    V = g.vector
+    off, on = engines(core)
+    roff, ron = engines(T.cores[r])
+    ow = S // 16
+    chunks = list(range(a, K, HELPERS))
+    g.iota(T.ip[:], [[0, 1]], 0, 1).then_inc(T.sem.gi, 1)
+    g.iota(T.ic[:, 0:ow], [[16, ow]], 0, 0).then_inc(T.sem.gi, 1)
+    V.wait_ge(T.sem.gi, 2)
+    v(V.tensor_scalar(out=T.q15[:], in0=T.ip[:], scalar1=15, scalar2=None, op0=op.bitwise_and))
+    vw()
+    v(V.tensor_copy(T.f15[:], T.q15[:]))
+    vw()
+    v(V.tensor_scalar(out=T.C[:, 0:ow], in0=T.ic[:, 0:ow], scalar1=T.f15[:], scalar2=None, op0=op.add))
+    V.wait_ge(T.sem.ls, len(ron))
+    for n, k in enumerate(chunks):
+        c0 = (TW * r) + ow * k
+        v(V.tensor_scalar(out=T.ti[:, n * ow:n * ow + ow], in0=T.LS[:, c0:c0 + ow], scalar1=12, scalar2=None,
+                          op0=op.arith_shift_right))
+    vw()
+    w = ow * len(chunks)
+    v(V.tensor_scalar(out=T.t1[:, 0:w], in0=T.ti[:, 0:w], scalar1=float(S), scalar2=None, op0=op.mult))
+    vw()
+    for n in range(len(chunks)):
+        v(V.tensor_tensor(T.t2[:, n * ow:n * ow + ow], T.t1[:, n * ow:n * ow + ow], T.C[:, 0:ow], op.add))
+    vw()
+    v(V.tensor_copy(T.O2[:, 0:w], T.t2[:, 0:w]))
+    vw()
+    sent = 0
+    for n, k in enumerate(chunks):
+        land = sum(len(first_hop(h, k)[r]) for h in range(N))
+        V.wait_ge(T.sem["h1_%d" % k], land)
+        V.tensor_copy(T.M[:, n * S:n * S + S],
+                      T.H[:, n * N * S:(n + 1) * N * S].indirect(T.O2[:, n * ow:n * ow + ow])
+                      ).then_inc(T.sem["mg%d" % k], 1)
+        g.wait_ge(T.sem["mg%d" % k], 1)
+        far = [c for i, c in enumerate(T.cores) if i != r]
+        here = T.F[:, r * L + k * S:r * L + k * S + S]
+        src = T.M[:, n * S:n * S + S]
+        g.remote_dma_fused([
+            RemoteDMATransfer(dst_ids=[dest(c) for c in far], dma_engine_mask=sum(off), remote_sem=T.sem.f2,
+                              srcs=[src], dsts=[here for c in far]),
+            RemoteDMATransfer(dst_ids=[dest(T.cores[r])], dma_engine_mask=sum(on), remote_sem=T.sem.f2,
+                              srcs=[src], dsts=[here])], local_sem=T.sem.lo)
+        sent += len(off) + len(on)
+    g.wait_ge(T.sem.lo, sent)

@@ -4,57 +4,79 @@ from concourse.mybir import AluOpType, ActivationFunctionType
 N, R, L = 4, 4096, 1024
 K = 4
 S = L // K
-HELPERS = 2
+OW = S // 16
+A, B, X = 0, 1, 2
+CHUNK = [(B, "lo"), (X, "two"), (B, "hi"), (A, "two")]
 SW, DW = L // 16, L // 128
 TW = SW + DW
-YB = 512
-NY = R // YB
+NS = N * DW
+YB = [256, 256, 512, 512, 768, 768, 512, 512]
+KW = R // 16
 
 SCRATCH = {
     "F": ("sbuf", [128, N * L + R], "float32"),
     "G": ("sbuf", [128, N * L], "float32"),
     "Y": ("sbuf", [128, R], "float32"),
-    "H": ("sbuf", [128, (K // HELPERS) * N * S], "float32"),
-    "M": ("sbuf", [128, (K // HELPERS) * S], "float32"),
+    "H": ("sbuf", [128, 2 * N * S], "float32"),
+    "M": ("sbuf", [128, 2 * S], "float32"),
     "LS": ("sbuf", [128, N * TW], "int32"),
     "O1": ("sbuf", [128, N * SW], "uint16"),
-    "O2": ("sbuf", [128, (K // HELPERS) * (S // 16)], "uint16"),
-    "O3": ("sbuf", [128, R // 16], "uint16"),
-    "DS": ("sbuf", [128, N * DW], "int32"),
-    "KI": ("sbuf", [128, N * DW], "int32"),
-    "BI": ("sbuf", [128, N * DW], "int32"),
-    "KD": ("sbuf", [128, N * DW], "float32"),
-    "BD": ("sbuf", [128, N * DW], "float32"),
-    "W": ("sbuf", [128, N * DW], "float32"),
-    "iw": ("sbuf", [128, N * DW], "int32"),
+    "O2": ("sbuf", [128, SW], "uint16"),
+    "O3": ("sbuf", [128, KW], "uint16"),
+    "DS": ("sbuf", [128, NS], "int32"),
+    "DQ": ("sbuf", [128, NS], "int32"),
+    "I9": ("sbuf", [128, NS], "int32"),
+    "I4": ("sbuf", [128, NS], "int32"),
+    "I0": ("sbuf", [128, NS], "int32"),
+    "F9": ("sbuf", [128, NS], "float32"),
+    "F0": ("sbuf", [128, NS], "float32"),
+    "KL": ("sbuf", [128, NS], "float32"),
+    "MD": ("sbuf", [128, NS], "float32"),
+    "W": ("sbuf", [128, NS], "float32"),
+    "iw": ("sbuf", [128, NS], "int32"),
     "ip": ("sbuf", [128, 1], "int32"),
+    "pm": ("sbuf", [128, 8], "float32"),
     "q15": ("sbuf", [128, 1], "int32"),
     "q7": ("sbuf", [128, 1], "int32"),
     "q3": ("sbuf", [128, 1], "int32"),
     "f15": ("sbuf", [128, 1], "float32"),
     "f7": ("sbuf", [128, 1], "float32"),
     "f3": ("sbuf", [128, 1], "float32"),
-    "ib": ("sbuf", [128, R // 16], "bfloat16"),
     "ia": ("sbuf", [128, 128], "bfloat16"),
-    "ic": ("sbuf", [128, R // 16], "int32"),
-    "C": ("sbuf", [128, R // 16], "float32"),
-    "A": ("sbuf", [128, N * DW * 128], "float16"),
-    "B": ("sbuf", [128, N * DW * (R // 16)], "float16"),
-    "t1": ("sbuf", [128, R // 16], "float32"),
-    "t2": ("sbuf", [128, R // 16], "float32"),
-    "t3": ("sbuf", [128, R // 16], "float32"),
-    "t4": ("sbuf", [128, R // 16], "float32"),
-    "t5": ("sbuf", [128, R // 16], "float32"),
-    "ti": ("sbuf", [128, 64], "int32"),
-    "ps": ("psum", [128, R // 16], "float32"),
+    "i16": ("sbuf", [128, 128], "bfloat16"),
+    "ic": ("sbuf", [128, KW], "int32"),
+    "C": ("sbuf", [128, KW], "float32"),
+    "A1": ("sbuf", [128, NS * 128], "float16"),
+    "B1": ("sbuf", [128, NS * 32], "float16"),
+    "SL": ("sbuf", [128, 8 * 128], "float16"),
+    "X1": ("sbuf", [128, 32], "float16"),
+    "t1": ("sbuf", [128, KW], "float32"),
+    "t2": ("sbuf", [128, KW], "float32"),
+    "t3": ("sbuf", [128, KW], "float32"),
+    "t4": ("sbuf", [128, KW], "float32"),
+    "t5": ("sbuf", [128, KW], "float32"),
+    "ti": ("sbuf", [128, SW], "int32"),
+    "tj": ("sbuf", [128, SW], "int32"),
+    "tk": ("sbuf", [128, SW], "int32"),
+    "p1": ("psum", [128, 32], "float32"),
+    "p2": ("psum", [128, KW], "float32"),
 }
-SEMAPHORES = (["ld", "gate", "tl", "ls", "o1", "lo", "o2", "f2", "gi", "vs", "mm", "o3", "st"]
+SEMAPHORES = (["ld", "gate", "tl", "ls", "o1", "lo", "f2", "gi", "vs", "mm", "m2", "o3", "st", "rl"]
               + ["ga%d" % k for k in range(K)] + ["h1_%d" % k for k in range(K)] + ["mg%d" % k for k in range(K)]
-              + ["oh%d" % r for r in range(N)] + ["fy%d" % j for j in range(NY)])
+              + ["oh%d" % r for r in range(N)] + ["fy%d" % j for j in range(len(YB))])
 
 
 def bits(m):
     return [1 << e for e in range(16) if (m >> e) & 1]
+
+
+def shares(off, how):
+    n = len(off)
+    if how == "lo":
+        return [[(1, off[:n // 2]), (2, off[n // 2:3 * n // 4]), (3, off[3 * n // 4:])]]
+    if how == "hi":
+        return [[(1, off[:n // 4]), (2, off[n // 4:n // 2]), (3, off[n // 2:])]]
+    return [[(1, off[:n // 2]), (2, off[n // 2:])], [(3, off)]]
 
 
 def rank_program(g, core, T, topo):
@@ -62,32 +84,20 @@ def rank_program(g, core, T, topo):
     V = g.vector
 
     def helpers(rc):
-        c = [x for x in range(256) if topo.host(x) == topo.host(rc) and topo.chip(x) == topo.chip(rc)
-             and topo.die(x) != topo.die(rc)]
-        return c[:HELPERS]
+        c = [x for x in range(256) if topo.host(x) == topo.host(rc) and topo.chip(x) == topo.chip(rc) and x != rc]
+        near = [x for x in c if topo.die(x) == topo.die(rc)]
+        far = [x for x in c if topo.die(x) != topo.die(rc)]
+        return [near[0], far[0], far[1]]
 
     def dest(dst):
         rid, pid = topo.addr(dst, core)
         return DstId(rid=rid, pnc=pid)
 
     def engines(src):
-        mine = [c for c in T.cores if topo.host(c) == topo.host(src) and topo.chip(c) == topo.chip(src)][0]
-        far = [c for c in T.cores if c != mine][0]
-        near = [c for c in helpers(mine) + [mine] if c != src][0]
-        off = topo.mask(src, far)
+        r = [i for i, c in enumerate(T.cores) if topo.host(c) == topo.host(src) and topo.chip(c) == topo.chip(src)][0]
+        near = [c for c in helpers(T.cores[r]) if c != src][0]
+        off = topo.mask(src, T.cores[(r + 1) % N])
         return bits(off), bits(topo.mask(src, near) & ~off)
-
-    def first_hop(h, k):
-        off, on = engines(T.cores[h])
-        rem = [(h + d) % N for d in range(1, N)]
-        n = len(off)
-        if k % 2 == 0:
-            cut = [off[:n // 2], off[n // 2:3 * n // 4], off[3 * n // 4:]]
-        else:
-            cut = [off[:n // 4], off[n // 4:n // 2], off[n // 2:]]
-        m = {rem[i]: cut[i] for i in range(N - 1)}
-        m[h] = on
-        return m
 
     cnt = [0]
 
@@ -102,7 +112,8 @@ def rank_program(g, core, T, topo):
     if q is None:
         own = [r for r in range(N) if core in helpers(T.cores[r])]
         if own:
-            helper_program(g, core, T, own[0], helpers(T.cores[own[0]]).index(core), dest, engines, first_hop, v, vw)
+            hs = [helpers(c) for c in T.cores]
+            helper_program(g, core, T, own[0], hs, dest, engines, v, vw)
         return
 
     off, on = engines(core)
@@ -123,15 +134,16 @@ def rank_program(g, core, T, topo):
                                           remote_sem=T.sem.ls, srcs=[tile], dsts=[tile for c in others])],
                        local_sem=T.sem.lo)
     g.sem_inc(T.sem.gate, 1)
-    g.remote_dma_fused([RemoteDMATransfer(dst_ids=[dest(c) for c in mine], dma_engine_mask=sum(on),
-                                          remote_sem=T.sem.ls, srcs=[tile], dsts=[tile for c in mine])],
-                       local_sem=T.sem.lo)
+    stile = T.LS[:, b:b + SW]
+    g.remote_dma_fused([RemoteDMATransfer(dst_ids=[dest(mine[A])], dma_engine_mask=sum(on),
+                                          remote_sem=T.sem.ls, srcs=[stile], dsts=[stile])], local_sem=T.sem.lo)
     sent = len(off) + len(on)
     g.iota(T.ip[:], [[0, 1]], 0, 1).then_inc(T.sem.gi, 1)
-    g.iota(T.ia[:], [[0, 8], [1, 16]], 0, 0, allow_small_or_imprecise_dtypes=True).then_inc(T.sem.gi, 1)
-    g.iota(T.ib[:], [[1, R // 16]], 0, 0, allow_small_or_imprecise_dtypes=True).then_inc(T.sem.gi, 1)
-    g.iota(T.ic[:], [[16, R // 16]], 0, 0).then_inc(T.sem.gi, 1)
-    hw = N * DW // 2
+    g.iota(T.pm[:], [[-16, 8]], 0, 1, allow_small_or_imprecise_dtypes=True).then_inc(T.sem.gi, 1)
+    g.iota(T.ia[:], [[1, 128]], 0, 0, allow_small_or_imprecise_dtypes=True).then_inc(T.sem.gi, 1)
+    g.iota(T.i16[:], [[0, 8], [1, 16]], 0, 0, allow_small_or_imprecise_dtypes=True).then_inc(T.sem.gi, 1)
+    g.iota(T.ic[:], [[16, KW]], 0, 0).then_inc(T.sem.gi, 1)
+    hw = NS // 2
     g.iota(T.iw[:, 0:hw], [[L, N // 2], [16, DW]], -2048, 0).then_inc(T.sem.gi, 1)
     g.iota(T.iw[:, hw:2 * hw], [[L, N // 2], [16, DW]], 1, 0).then_inc(T.sem.gi, 1)
 
@@ -140,8 +152,7 @@ def rank_program(g, core, T, topo):
                         scalar2=float(R - 1), op0=op.subtract, op1=op.min).then_inc(T.sem.o1, 1)
     V.wait_ge(T.sem.ld, 144)
     offsets(q)
-    arrive = (N - 1) * len(off)
-    V.wait_ge(T.sem.ls, arrive)
+    V.wait_ge(T.sem.ls, (N - 1) * len(off))
     for r in range(N):
         if r != q:
             offsets(r)
@@ -150,70 +161,93 @@ def rank_program(g, core, T, topo):
     g.scalar.wait_ge(T.sem.o1, N)
     g.scalar.wait_ge(T.sem.tl, 32)
     win = T.F[:, N * L:N * L + R]
-    ow = S // 16
-    for k in range(K):
-        for r in range(N):
-            idx = T.O1[:, SW * r + ow * k:SW * r + ow * k + ow]
-            out = T.G[:, (k * N + r) * S:(k * N + r + 1) * S]
-            if r < N // 2:
-                V.tensor_copy(out, win.indirect(idx)).then_inc(T.sem["ga%d" % k], 1)
-            else:
-                g.scalar.activation(out, win.indirect(idx), ActivationFunctionType.Copy).then_inc(T.sem["ga%d" % k], 1)
-    for k in range(K):
-        plan = first_hop(q, k)
-        g.wait_ge(T.sem["ga%d" % k], N)
-        n = k // HELPERS
-        tr = []
-        for d in list(range(1, N)) + [0]:
-            r = (q + d) % N
-            hc = helpers(T.cores[r])[k % HELPERS]
-            tr.append(RemoteDMATransfer(dst_ids=[dest(hc)], dma_engine_mask=sum(plan[r]), remote_sem=T.sem["h1_%d" % k],
-                                        srcs=[T.G[:, (k * N + r) * S:(k * N + r + 1) * S]],
-                                        dsts=[T.H[:, (n * N + q) * S:(n * N + q + 1) * S]]))
-            sent += len(plan[r])
-        g.remote_dma_fused(tr, local_sem=T.sem.lo)
 
-    V.wait_ge(T.sem.gi, 6)
+    def cand(k, d):
+        c = (k * N + (d - 1) % N) * S
+        return T.G[:, c:c + S]
+    for k in range(K):
+        for d in range(N):
+            r = (q + d) % N
+            idx = T.O1[:, SW * r + OW * k:SW * r + OW * k + OW]
+            if d < N // 2:
+                V.tensor_copy(cand(k, d), win.indirect(idx)).then_inc(T.sem["ga%d" % k], 1)
+            else:
+                g.scalar.activation(cand(k, d), win.indirect(idx),
+                                    ActivationFunctionType.Copy).then_inc(T.sem["ga%d" % k], 1)
+    for k in range(K):
+        who, how = CHUNK[k]
+        g.wait_ge(T.sem["ga%d" % k], N)
+        if who == X:
+            g.remote_dma_fused([RemoteDMATransfer(dst_ids=[dest(mine[X])], dma_engine_mask=sum(on),
+                                                  remote_sem=T.sem.rl, srcs=[T.G[:, k * N * S:(k + 1) * N * S]],
+                                                  dsts=[T.H[:, 0:N * S]])], local_sem=T.sem.lo)
+            sent += len(on)
+            continue
+        n = [j for j in range(K) if CHUNK[j][0] == who].index(k)
+        for i, call in enumerate(shares(off, how)):
+            tr = []
+            for d, eng in call + ([(0, on)] if i == 0 else []):
+                hc = helpers(T.cores[(q + d) % N])[who]
+                c = (n * N + (-d) % N) * S
+                tr.append(RemoteDMATransfer(dst_ids=[dest(hc)], dma_engine_mask=sum(eng),
+                                            remote_sem=T.sem["h1_%d" % k], srcs=[cand(k, d)],
+                                            dsts=[T.H[:, c:c + S]]))
+                sent += len(eng)
+            g.remote_dma_fused(tr, local_sem=T.sem.lo)
+
+    V.wait_ge(T.sem.gi, 7)
     v(V.tensor_scalar(out=T.q15[:], in0=T.ip[:], scalar1=15, scalar2=None, op0=op.bitwise_and))
     v(V.tensor_scalar(out=T.q7[:], in0=T.ip[:], scalar1=7, scalar2=None, op0=op.bitwise_and))
     v(V.tensor_scalar(out=T.q3[:], in0=T.ip[:], scalar1=3, scalar2=None, op0=op.arith_shift_right))
     for r in range(N):
-        v(V.tensor_copy(T.DS[:, DW * r:DW * r + DW], T.LS[:, TW * r + SW:TW * r + TW]))
+        v(V.tensor_scalar(out=T.DQ[:, DW * r:DW * r + DW], in0=T.LS[:, TW * r + SW:TW * r + TW],
+                          scalar1=float(R * q), scalar2=None, op0=op.subtract))
     vw()
     v(V.tensor_copy(T.f15[:], T.q15[:]))
     v(V.tensor_scalar(out=T.f7[:], in0=T.q7[:], scalar1=128.0, scalar2=None, op0=op.mult))
     v(V.tensor_copy(T.f3[:], T.q3[:]))
-    v(V.tensor_scalar(out=T.KI[:], in0=T.DS[:], scalar1=4, scalar2=None, op0=op.arith_shift_right))
-    v(V.tensor_scalar(out=T.BI[:], in0=T.DS[:], scalar1=15, scalar2=None, op0=op.bitwise_and))
+    v(V.tensor_scalar(out=T.I9[:], in0=T.DQ[:], scalar1=9, scalar2=None, op0=op.arith_shift_right))
+    v(V.tensor_scalar(out=T.I4[:], in0=T.DQ[:], scalar1=4, scalar2=31, op0=op.arith_shift_right, op1=op.bitwise_and))
+    v(V.tensor_scalar(out=T.I0[:], in0=T.DQ[:], scalar1=15, scalar2=None, op0=op.bitwise_and))
     vw()
-    v(V.tensor_scalar(out=T.C[:], in0=T.ic[:], scalar1=T.f15[:], scalar2=float(N * L - 2048), op0=op.add, op1=op.add))
+    v(V.tensor_scalar(out=T.F9[:], in0=T.I9[:], scalar1=16.0, scalar2=None, op0=op.mult))
+    v(V.tensor_copy(T.F0[:], T.I0[:]))
+    v(V.tensor_copy(T.KL[:], T.I4[:]))
     v(V.tensor_scalar(out=T.W[:], in0=T.iw[:], scalar1=T.f7[:], scalar2=T.f3[:], op0=op.add, op1=op.add))
-    v(V.tensor_scalar(out=T.KD[:], in0=T.KI[:], scalar1=float(q * R // 16), scalar2=None, op0=op.subtract))
-    v(V.tensor_copy(T.BD[:], T.BI[:]))
     vw()
-    kw = R // 16
+    v(V.tensor_tensor(T.MD[:], T.F9[:], T.F0[:], op.add))
+    vw()
     for r in range(N):
         s = T.sem["oh%d" % r]
-        for u in range(DW):
-            c = r * DW + u
-            V.tensor_scalar(out=T.A[:, 128 * c:128 * c + 128], in0=T.ia[:], scalar1=T.BD[:, c:c + 1],
+        for c in range(r * DW, r * DW + DW):
+            V.tensor_scalar(out=T.A1[:, 128 * c:128 * c + 128], in0=T.ia[:], scalar1=T.MD[:, c:c + 1],
                             scalar2=T.W[:, c:c + 1], op0=op.is_equal, op1=op.mult).then_inc(s, 1)
-            V.tensor_scalar(out=T.B[:, kw * c:kw * c + kw], in0=T.ib[:], scalar1=T.KD[:, c:c + 1],
+            V.tensor_scalar(out=T.B1[:, 32 * c:32 * c + 32], in0=T.ia[:, 0:32], scalar1=T.KL[:, c:c + 1],
                             scalar2=None, op0=op.is_equal).then_inc(s, 1)
     for r in range(N):
         g.tensor.wait_ge(T.sem["oh%d" % r], 2 * DW)
-        for u in range(DW):
-            c = r * DW + u
-            last = c == N * DW - 1
-            ins = g.tensor.matmul(T.ps[:], T.A[:, 128 * c:128 * c + 128], T.B[:, kw * c:kw * c + kw], c == 0, last)
+        for c in range(r * DW, r * DW + DW):
+            last = c == NS - 1
+            ins = g.tensor.matmul(T.p1[:], T.A1[:, 128 * c:128 * c + 128], T.B1[:, 32 * c:32 * c + 32], c == 0, last)
             if last:
                 ins.then_inc(T.sem.mm, 1)
+    for kh in range(8):
+        v(V.tensor_scalar(out=T.SL[:, 128 * kh:128 * kh + 128], in0=T.i16[:], scalar1=T.pm[:, kh:kh + 1],
+                          scalar2=None, op0=op.is_equal))
+    v(V.tensor_scalar(out=T.C[:], in0=T.ic[:], scalar1=T.f15[:], scalar2=float(N * L - 2048), op0=op.add, op1=op.add))
     V.wait_ge(T.sem.mm, 1)
-    v(V.tensor_scalar(out=T.t1[:], in0=T.ps[:], scalar1=0.0, scalar2=None, op0=op.is_equal))
-    v(V.tensor_scalar(out=T.t2[:], in0=T.ps[:], scalar1=0.0, scalar2=2047.0, op0=op.is_le, op1=op.add))
+    v(V.tensor_copy(T.X1[:], T.p1[:]))
+    g.tensor.wait_ge(T.sem.vs, cnt[0])
+    for kh in range(8):
+        g.tensor.matmul(T.p2[:, 32 * kh:32 * kh + 32], T.SL[:, 128 * kh:128 * kh + 128], T.X1[:], True,
+                        True).then_inc(T.sem.m2, 1)
+    vw()
+    V.wait_ge(T.sem.m2, 8)
+    v(V.tensor_scalar(out=T.t1[:], in0=T.p2[:], scalar1=0.0, scalar2=None, op0=op.is_equal))
+    v(V.tensor_scalar(out=T.t2[:], in0=T.p2[:], scalar1=0.0, scalar2=2047.0, op0=op.is_le, op1=op.add))
     vw()
     v(V.tensor_tensor(T.t3[:], T.t1[:], T.C[:], op.mult))
-    v(V.tensor_tensor(T.t4[:], T.t2[:], T.ps[:], op.add))
+    v(V.tensor_tensor(T.t4[:], T.t2[:], T.p2[:], op.add))
     vw()
     v(V.tensor_tensor(T.t5[:], T.t3[:], T.t4[:], op.add))
     vw()
@@ -221,63 +255,88 @@ def rank_program(g, core, T, topo):
     land = 0
     for r in range(N):
         for k in range(K):
-            o2, n2 = engines(helpers(T.cores[r])[k % HELPERS])
+            o2, n2 = engines(helpers(T.cores[r])[CHUNK[k][0]])
             land += len(n2) if r == q else len(o2)
     for e in (V, g.scalar):
         e.wait_ge(T.sem.o3, 1)
         e.wait_ge(T.sem.f2, land)
-    yw = YB // 16
-    for j in range(NY):
-        src = T.F[:].indirect(T.O3[:, yw * j:yw * j + yw])
-        out = T.Y[:, YB * j:YB * j + YB]
+    c = 0
+    for j, w in enumerate(YB):
+        src = T.F[:].indirect(T.O3[:, c // 16:(c + w) // 16])
         s = T.sem["fy%d" % j]
         if j % 2 == 0:
-            V.tensor_copy(out, src).then_inc(s, 1)
+            V.tensor_copy(T.Y[:, c:c + w], src).then_inc(s, 1)
         else:
-            g.scalar.activation(out, src, ActivationFunctionType.Copy).then_inc(s, 1)
-    for j in range(NY):
-        g.sync.wait_ge(T.sem["fy%d" % j], 1)
-        g.sync.dma_start(T.y[:, YB * j:YB * j + YB], T.Y[:, YB * j:YB * j + YB]).then_inc(T.sem.st, 16)
-    g.sync.wait_ge(T.sem.st, 16 * NY)
+            g.scalar.activation(T.Y[:, c:c + w], src, ActivationFunctionType.Copy).then_inc(s, 1)
+        g.sync.wait_ge(s, 1)
+        g.sync.dma_start(T.y[:, c:c + w], T.Y[:, c:c + w]).then_inc(T.sem.st, 16)
+        c += w
+    g.sync.wait_ge(T.sem.st, 16 * len(YB))
     g.wait_ge(T.sem.lo, sent)
 
 
-def helper_program(g, core, T, r, a, dest, engines, first_hop, v, vw):
+def helper_program(g, core, T, r, hs, dest, engines, v, vw):
     op = AluOpType
     V = g.vector
+    me = hs[r].index(core)
     off, on = engines(core)
     roff, ron = engines(T.cores[r])
-    ow = S // 16
-    chunks = list(range(a, K, HELPERS))
+    chunks = [k for k in range(K) if CHUNK[k][0] == me]
+    sent = 0
+    heard = {A: len(ron), X: len(off), B: len(off)}[me]
+    stile = T.LS[:, TW * r:TW * r + SW]
+    if me in (A, X):
+        g.wait_ge(T.sem.ls, heard)
+        g.remote_dma_fused([RemoteDMATransfer(dst_ids=[dest(hs[r][X if me == A else B])], dma_engine_mask=sum(off),
+                                              remote_sem=T.sem.ls, srcs=[stile], dsts=[stile])], local_sem=T.sem.lo)
+        sent += len(off)
     g.iota(T.ip[:], [[0, 1]], 0, 1).then_inc(T.sem.gi, 1)
-    g.iota(T.ic[:, 0:ow], [[16, ow]], 0, 0).then_inc(T.sem.gi, 1)
+    g.iota(T.ic[:, 0:OW], [[16, OW]], 0, 0).then_inc(T.sem.gi, 1)
+    if me == X:
+        k = chunks[0]
+        g.wait_ge(T.sem.rl, len(ron))
+        for call in shares(off, CHUNK[k][1]):
+            tr = []
+            for d, eng in call:
+                c = (N - 1 + (-d) % N) * S
+                tr.append(RemoteDMATransfer(dst_ids=[dest(hs[(r + d) % N][X])], dma_engine_mask=sum(eng),
+                                            remote_sem=T.sem["h1_%d" % k], srcs=[T.H[:, (d - 1) * S:d * S]],
+                                            dsts=[T.H[:, c:c + S]]))
+                sent += len(eng)
+            g.remote_dma_fused(tr, local_sem=T.sem.lo)
     V.wait_ge(T.sem.gi, 2)
     v(V.tensor_scalar(out=T.q15[:], in0=T.ip[:], scalar1=15, scalar2=None, op0=op.bitwise_and))
     vw()
     v(V.tensor_copy(T.f15[:], T.q15[:]))
     vw()
-    v(V.tensor_scalar(out=T.C[:, 0:ow], in0=T.ic[:, 0:ow], scalar1=T.f15[:], scalar2=None, op0=op.add))
-    V.wait_ge(T.sem.ls, len(ron))
+    v(V.tensor_scalar(out=T.C[:, 0:OW], in0=T.ic[:, 0:OW], scalar1=T.f15[:], scalar2=None, op0=op.add))
+    V.wait_ge(T.sem.ls, heard)
+    v(V.tensor_scalar(out=T.ti[:], in0=stile, scalar1=12, scalar2=None, op0=op.arith_shift_right))
+    vw()
+    v(V.tensor_scalar(out=T.tj[:], in0=T.ti[:], scalar1=float(N - r), scalar2=None, op0=op.add))
+    vw()
+    v(V.tensor_scalar(out=T.tk[:], in0=T.tj[:], scalar1=N - 1, scalar2=None, op0=op.bitwise_and))
+    vw()
+    v(V.tensor_scalar(out=T.t1[:, 0:SW], in0=T.tk[:], scalar1=float(S), scalar2=None, op0=op.mult))
+    vw()
+    for k in chunks:
+        v(V.tensor_tensor(T.t2[:, k * OW:k * OW + OW], T.t1[:, k * OW:k * OW + OW], T.C[:, 0:OW], op.add))
+    vw()
+    for k in chunks:
+        v(V.tensor_copy(T.O2[:, k * OW:k * OW + OW], T.t2[:, k * OW:k * OW + OW]))
+    vw()
     for n, k in enumerate(chunks):
-        c0 = (TW * r) + ow * k
-        v(V.tensor_scalar(out=T.ti[:, n * ow:n * ow + ow], in0=T.LS[:, c0:c0 + ow], scalar1=12, scalar2=None,
-                          op0=op.arith_shift_right))
-    vw()
-    w = ow * len(chunks)
-    v(V.tensor_scalar(out=T.t1[:, 0:w], in0=T.ti[:, 0:w], scalar1=float(S), scalar2=None, op0=op.mult))
-    vw()
-    for n in range(len(chunks)):
-        v(V.tensor_tensor(T.t2[:, n * ow:n * ow + ow], T.t1[:, n * ow:n * ow + ow], T.C[:, 0:ow], op.add))
-    vw()
-    v(V.tensor_copy(T.O2[:, 0:w], T.t2[:, 0:w]))
-    vw()
-    sent = 0
-    for n, k in enumerate(chunks):
-        land = sum(len(first_hop(h, k)[r]) for h in range(N))
+        who, how = CHUNK[k]
+        land = sum(len(eng) for call in shares(roff, how) for d, eng in call)
+        if me == X:
+            V.wait_ge(T.sem.rl, len(ron))
+            c = (N - 1) * S
+        else:
+            land += len(ron)
+            c = n * N * S
         V.wait_ge(T.sem["h1_%d" % k], land)
         V.tensor_copy(T.M[:, n * S:n * S + S],
-                      T.H[:, n * N * S:(n + 1) * N * S].indirect(T.O2[:, n * ow:n * ow + ow])
-                      ).then_inc(T.sem["mg%d" % k], 1)
+                      T.H[:, c:c + N * S].indirect(T.O2[:, k * OW:k * OW + OW])).then_inc(T.sem["mg%d" % k], 1)
         g.wait_ge(T.sem["mg%d" % k], 1)
         far = [c for i, c in enumerate(T.cores) if i != r]
         here = T.F[:, r * L + k * S:r * L + k * S + S]

@@ -2,14 +2,15 @@ from concourse.bass import DstId, RemoteDMATransfer
 from concourse.mybir import AluOpType, ActivationFunctionType
 
 N, R, L = 4, 4096, 1024
-K = 4
-S = L // K
-OW = S // 16
-A, B, X = 0, 1, 2
-CHUNK = [(B, "lo"), (X, "two"), (B, "hi"), (A, "two")]
+A, B, X, Z = 0, 1, 2, 3
+CHUNK = [(352, 0, B, "lo"), (160, 512, X, "two"), (160, 352, Z, "two"), (352, 672, A, "hi")]
+K = len(CHUNK)
+SMAX = max(c[0] for c in CHUNK)
 SW, DW = L // 16, L // 128
 TW = SW + DW
+HW = SW // 2
 NS = N * DW
+TB = [2048, 1024, 1024]
 YB = [256, 256, 512, 512, 768, 768, 512, 512]
 KW = R // 16
 
@@ -17,13 +18,12 @@ SCRATCH = {
     "F": ("sbuf", [128, N * L + R], "float32"),
     "G": ("sbuf", [128, N * L], "float32"),
     "Y": ("sbuf", [128, R], "float32"),
-    "H": ("sbuf", [128, 2 * N * S], "float32"),
-    "M": ("sbuf", [128, 2 * S], "float32"),
+    "H": ("sbuf", [128, (2 * N - 1) * SMAX], "float32"),
+    "M": ("sbuf", [128, SMAX], "float32"),
     "LS": ("sbuf", [128, N * TW], "int32"),
     "O1": ("sbuf", [128, N * SW], "uint16"),
     "O2": ("sbuf", [128, SW], "uint16"),
     "O3": ("sbuf", [128, KW], "uint16"),
-    "DS": ("sbuf", [128, NS], "int32"),
     "DQ": ("sbuf", [128, NS], "int32"),
     "I9": ("sbuf", [128, NS], "int32"),
     "I4": ("sbuf", [128, NS], "int32"),
@@ -61,9 +61,8 @@ SCRATCH = {
     "p1": ("psum", [128, 32], "float32"),
     "p2": ("psum", [128, KW], "float32"),
 }
-SEMAPHORES = (["ld", "gate", "tl", "ls", "o1", "lo", "f2", "gi", "vs", "mm", "m2", "o3", "st", "rl"]
-              + ["ga%d" % k for k in range(K)] + ["h1_%d" % k for k in range(K)] + ["mg%d" % k for k in range(K)]
-              + ["oh%d" % r for r in range(N)] + ["fy%d" % j for j in range(len(YB))])
+SEMAPHORES = (["ld", "gate", "tl", "ls", "l2", "o1", "lo", "f2", "gi", "vs", "mm", "m2", "o3", "st", "rl", "h1", "mg"]
+              + ["ga%d" % k for k in range(K)] + ["oh%d" % r for r in range(N)] + ["fy%d" % j for j in range(len(YB))])
 
 
 def bits(m):
@@ -87,7 +86,7 @@ def rank_program(g, core, T, topo):
         c = [x for x in range(256) if topo.host(x) == topo.host(rc) and topo.chip(x) == topo.chip(rc) and x != rc]
         near = [x for x in c if topo.die(x) == topo.die(rc)]
         far = [x for x in c if topo.die(x) != topo.die(rc)]
-        return [near[0], far[0], far[1]]
+        return [near[0], far[0], far[1], far[2]]
 
     def dest(dst):
         rid, pid = topo.addr(dst, core)
@@ -113,124 +112,144 @@ def rank_program(g, core, T, topo):
         own = [r for r in range(N) if core in helpers(T.cores[r])]
         if own:
             hs = [helpers(c) for c in T.cores]
-            helper_program(g, core, T, own[0], hs, dest, engines, v, vw)
+            helper_program(g, core, T, own[0], hs, dest, engines, v, vw, cnt)
         return
 
     off, on = engines(core)
-    others = [c for c in T.cores if c != core]
+    others = [T.cores[(q + d) % N] for d in range(1, N)]
     mine = helpers(core)
     b = TW * q
     for a in range(8):
         e = g.sync if a % 2 == 0 else g.scalar
         e.dma_start(T.LS[16 * a:16 * a + 16, b:b + SW], T.src[:]).then_inc(T.sem.ld, 16)
     g.scalar.dma_start(T.LS[:, b + SW:b + TW], T.dst[:]).then_inc(T.sem.ld, 16)
-    half = R // 2
-    g.sync.dma_start(T.F[:, N * L:N * L + half], T.tab[:, 0:half]).then_inc(T.sem.tl, 16)
-    g.sync.wait_ge(T.sem.gate, 1)
-    g.sync.dma_start(T.F[:, N * L + half:N * L + R], T.tab[:, half:R]).then_inc(T.sem.tl, 16)
+    a = 0
+    for j, w in enumerate(TB):
+        if j == 1:
+            g.sync.wait_ge(T.sem.ld, 144)
+        if j == 2:
+            g.sync.wait_ge(T.sem.gate, 1)
+        g.sync.dma_start(T.F[:, N * L + a:N * L + a + w], T.tab[:, a:a + w]).then_inc(T.sem.tl, 16)
+        a += w
+    g.iota(T.ip[:], [[0, 1]], 0, 1).then_inc(T.sem.gi, 1)
+    hw = NS // 2
+    g.iota(T.iw[:, 0:hw], [[L, N // 2], [16, DW]], -2048, 0).then_inc(T.sem.gi, 1)
+    g.iota(T.iw[:, hw:2 * hw], [[L, N // 2], [16, DW]], 1, 0).then_inc(T.sem.gi, 1)
+    g.iota(T.ia[:], [[1, 128]], 0, 0, allow_small_or_imprecise_dtypes=True).then_inc(T.sem.gi, 1)
     tile = T.LS[:, b:b + TW]
     g.wait_ge(T.sem.ld, 144)
     g.remote_dma_fused([RemoteDMATransfer(dst_ids=[dest(c) for c in others], dma_engine_mask=sum(off),
                                           remote_sem=T.sem.ls, srcs=[tile], dsts=[tile for c in others])],
                        local_sem=T.sem.lo)
     g.sem_inc(T.sem.gate, 1)
-    stile = T.LS[:, b:b + SW]
-    g.remote_dma_fused([RemoteDMATransfer(dst_ids=[dest(mine[A])], dma_engine_mask=sum(on),
-                                          remote_sem=T.sem.ls, srcs=[stile], dsts=[stile])], local_sem=T.sem.lo)
+    h = len(on) // 2
+    g.remote_dma_fused([RemoteDMATransfer(dst_ids=[dest(mine[who])], dma_engine_mask=sum(eng), remote_sem=T.sem.ls,
+                                          srcs=[T.LS[:, c:c + HW]], dsts=[T.LS[:, c:c + HW]])
+                        for who, eng, c in ((A, on[:h], b), (Z, on[h:], b + HW))], local_sem=T.sem.lo)
     sent = len(off) + len(on)
-    g.iota(T.ip[:], [[0, 1]], 0, 1).then_inc(T.sem.gi, 1)
     g.iota(T.pm[:], [[-16, 8]], 0, 1, allow_small_or_imprecise_dtypes=True).then_inc(T.sem.gi, 1)
-    g.iota(T.ia[:], [[1, 128]], 0, 0, allow_small_or_imprecise_dtypes=True).then_inc(T.sem.gi, 1)
     g.iota(T.i16[:], [[0, 8], [1, 16]], 0, 0, allow_small_or_imprecise_dtypes=True).then_inc(T.sem.gi, 1)
     g.iota(T.ic[:], [[16, KW]], 0, 0).then_inc(T.sem.gi, 1)
-    hw = NS // 2
-    g.iota(T.iw[:, 0:hw], [[L, N // 2], [16, DW]], -2048, 0).then_inc(T.sem.gi, 1)
-    g.iota(T.iw[:, hw:2 * hw], [[L, N // 2], [16, DW]], 1, 0).then_inc(T.sem.gi, 1)
 
     def offsets(r):
         V.tensor_scalar(out=T.O1[:, SW * r:SW * r + SW], in0=T.LS[:, TW * r:TW * r + SW], scalar1=float(R * q),
                         scalar2=float(R - 1), op0=op.subtract, op1=op.min).then_inc(T.sem.o1, 1)
-    V.wait_ge(T.sem.ld, 144)
-    offsets(q)
-    V.wait_ge(T.sem.ls, (N - 1) * len(off))
-    for r in range(N):
-        if r != q:
-            offsets(r)
-    V.wait_ge(T.sem.o1, N)
-    V.wait_ge(T.sem.tl, 32)
-    g.scalar.wait_ge(T.sem.o1, N)
-    g.scalar.wait_ge(T.sem.tl, 32)
-    win = T.F[:, N * L:N * L + R]
 
-    def cand(k, d):
-        c = (k * N + (d - 1) % N) * S
-        return T.G[:, c:c + S]
-    for k in range(K):
-        for d in range(N):
-            r = (q + d) % N
-            idx = T.O1[:, SW * r + OW * k:SW * r + OW * k + OW]
-            if d < N // 2:
-                V.tensor_copy(cand(k, d), win.indirect(idx)).then_inc(T.sem["ga%d" % k], 1)
-            else:
-                g.scalar.activation(cand(k, d), win.indirect(idx),
-                                    ActivationFunctionType.Copy).then_inc(T.sem["ga%d" % k], 1)
-    for k in range(K):
-        who, how = CHUNK[k]
-        g.wait_ge(T.sem["ga%d" % k], N)
-        if who == X:
-            g.remote_dma_fused([RemoteDMATransfer(dst_ids=[dest(mine[X])], dma_engine_mask=sum(on),
-                                                  remote_sem=T.sem.rl, srcs=[T.G[:, k * N * S:(k + 1) * N * S]],
-                                                  dsts=[T.H[:, 0:N * S]])], local_sem=T.sem.lo)
-            sent += len(on)
-            continue
-        n = [j for j in range(K) if CHUNK[j][0] == who].index(k)
-        for i, call in enumerate(shares(off, how)):
-            tr = []
-            for d, eng in call + ([(0, on)] if i == 0 else []):
-                hc = helpers(T.cores[(q + d) % N])[who]
-                c = (n * N + (-d) % N) * S
-                tr.append(RemoteDMATransfer(dst_ids=[dest(hc)], dma_engine_mask=sum(eng),
-                                            remote_sem=T.sem["h1_%d" % k], srcs=[cand(k, d)],
-                                            dsts=[T.H[:, c:c + S]]))
-                sent += len(eng)
-            g.remote_dma_fused(tr, local_sem=T.sem.lo)
+    def digits(c, n):
+        z = slice(c, c + n)
+        for r in range(c // DW, (c + n) // DW):
+            v(V.tensor_scalar(out=T.DQ[:, DW * r:DW * r + DW], in0=T.LS[:, TW * r + SW:TW * r + TW],
+                              scalar1=float(R * q), scalar2=None, op0=op.subtract))
+        vw()
+        v(V.tensor_scalar(out=T.I9[:, z], in0=T.DQ[:, z], scalar1=9, scalar2=None, op0=op.arith_shift_right))
+        v(V.tensor_scalar(out=T.I0[:, z], in0=T.DQ[:, z], scalar1=15, scalar2=None, op0=op.bitwise_and))
+        v(V.tensor_scalar(out=T.I4[:, z], in0=T.DQ[:, z], scalar1=4, scalar2=31, op0=op.arith_shift_right,
+                          op1=op.bitwise_and))
+        vw()
+        v(V.tensor_scalar(out=T.F9[:, z], in0=T.I9[:, z], scalar1=16.0, scalar2=None, op0=op.mult))
+        v(V.tensor_copy(T.F0[:, z], T.I0[:, z]))
+        v(V.tensor_copy(T.KL[:, z], T.I4[:, z]))
+        vw()
+        v(V.tensor_tensor(T.MD[:, z], T.F9[:, z], T.F0[:, z], op.add))
+        vw()
 
-    V.wait_ge(T.sem.gi, 7)
-    v(V.tensor_scalar(out=T.q15[:], in0=T.ip[:], scalar1=15, scalar2=None, op0=op.bitwise_and))
-    v(V.tensor_scalar(out=T.q7[:], in0=T.ip[:], scalar1=7, scalar2=None, op0=op.bitwise_and))
-    v(V.tensor_scalar(out=T.q3[:], in0=T.ip[:], scalar1=3, scalar2=None, op0=op.arith_shift_right))
-    for r in range(N):
-        v(V.tensor_scalar(out=T.DQ[:, DW * r:DW * r + DW], in0=T.LS[:, TW * r + SW:TW * r + TW],
-                          scalar1=float(R * q), scalar2=None, op0=op.subtract))
-    vw()
-    v(V.tensor_copy(T.f15[:], T.q15[:]))
-    v(V.tensor_scalar(out=T.f7[:], in0=T.q7[:], scalar1=128.0, scalar2=None, op0=op.mult))
-    v(V.tensor_copy(T.f3[:], T.q3[:]))
-    v(V.tensor_scalar(out=T.I9[:], in0=T.DQ[:], scalar1=9, scalar2=None, op0=op.arith_shift_right))
-    v(V.tensor_scalar(out=T.I4[:], in0=T.DQ[:], scalar1=4, scalar2=31, op0=op.arith_shift_right, op1=op.bitwise_and))
-    v(V.tensor_scalar(out=T.I0[:], in0=T.DQ[:], scalar1=15, scalar2=None, op0=op.bitwise_and))
-    vw()
-    v(V.tensor_scalar(out=T.F9[:], in0=T.I9[:], scalar1=16.0, scalar2=None, op0=op.mult))
-    v(V.tensor_copy(T.F0[:], T.I0[:]))
-    v(V.tensor_copy(T.KL[:], T.I4[:]))
-    v(V.tensor_scalar(out=T.W[:], in0=T.iw[:], scalar1=T.f7[:], scalar2=T.f3[:], op0=op.add, op1=op.add))
-    vw()
-    v(V.tensor_tensor(T.MD[:], T.F9[:], T.F0[:], op.add))
-    vw()
-    for r in range(N):
+    def onehot(r):
         s = T.sem["oh%d" % r]
         for c in range(r * DW, r * DW + DW):
             V.tensor_scalar(out=T.A1[:, 128 * c:128 * c + 128], in0=T.ia[:], scalar1=T.MD[:, c:c + 1],
                             scalar2=T.W[:, c:c + 1], op0=op.is_equal, op1=op.mult).then_inc(s, 1)
             V.tensor_scalar(out=T.B1[:, 32 * c:32 * c + 32], in0=T.ia[:, 0:32], scalar1=T.KL[:, c:c + 1],
                             scalar2=None, op0=op.is_equal).then_inc(s, 1)
+
+    V.wait_ge(T.sem.ld, 144)
+    offsets(q)
+    V.wait_ge(T.sem.gi, 4)
+    v(V.tensor_scalar(out=T.q15[:], in0=T.ip[:], scalar1=15, scalar2=None, op0=op.bitwise_and))
+    v(V.tensor_scalar(out=T.q7[:], in0=T.ip[:], scalar1=7, scalar2=None, op0=op.bitwise_and))
+    v(V.tensor_scalar(out=T.q3[:], in0=T.ip[:], scalar1=3, scalar2=None, op0=op.arith_shift_right))
+    vw()
+    v(V.tensor_copy(T.f15[:], T.q15[:]))
+    v(V.tensor_scalar(out=T.f7[:], in0=T.q7[:], scalar1=128.0, scalar2=None, op0=op.mult))
+    v(V.tensor_copy(T.f3[:], T.q3[:]))
+    vw()
+    v(V.tensor_scalar(out=T.W[:], in0=T.iw[:], scalar1=T.f7[:], scalar2=T.f3[:], op0=op.add, op1=op.add))
+    digits(q * DW, DW)
+    onehot(q)
+    V.wait_ge(T.sem.ls, (N - 1) * len(off))
     for r in range(N):
+        if r != q:
+            offsets(r)
+    V.wait_ge(T.sem.o1, N)
+    V.wait_ge(T.sem.tl, 16 * len(TB))
+    g.scalar.wait_ge(T.sem.o1, N)
+    g.scalar.wait_ge(T.sem.tl, 16 * len(TB))
+    win = T.F[:, N * L:N * L + R]
+
+    def cand(k, d):
+        size, slot = CHUNK[k][:2]
+        c = N * slot + (d - 1) % N * size
+        return T.G[:, c:c + size]
+    for k in range(K):
+        size, slot = CHUNK[k][:2]
+        for d in range(N):
+            c = SW * ((q + d) % N) + slot // 16
+            idx = T.O1[:, c:c + size // 16]
+            if d < N // 2:
+                V.tensor_copy(cand(k, d), win.indirect(idx)).then_inc(T.sem["ga%d" % k], 1)
+            else:
+                g.scalar.activation(cand(k, d), win.indirect(idx),
+                                    ActivationFunctionType.Copy).then_inc(T.sem["ga%d" % k], 1)
+    for k in range(K):
+        size, slot, who, how = CHUNK[k]
+        g.wait_ge(T.sem["ga%d" % k], N)
+        if who in (X, Z):
+            g.remote_dma_fused([RemoteDMATransfer(dst_ids=[dest(mine[who])], dma_engine_mask=sum(on),
+                                                  remote_sem=T.sem.rl, srcs=[T.G[:, N * slot:N * (slot + size)]],
+                                                  dsts=[T.H[:, 0:N * size]])], local_sem=T.sem.lo)
+            sent += len(on)
+            continue
+        for i, call in enumerate(shares(off, how)):
+            tr = []
+            for d, eng in call + ([(0, on)] if i == 0 else []):
+                hc = helpers(T.cores[(q + d) % N])[who]
+                c = (N - 1 + (-d) % N) * size
+                tr.append(RemoteDMATransfer(dst_ids=[dest(hc)], dma_engine_mask=sum(eng), remote_sem=T.sem.h1,
+                                            srcs=[cand(k, d)], dsts=[T.H[:, c:c + size]]))
+                sent += len(eng)
+            g.remote_dma_fused(tr, local_sem=T.sem.lo)
+
+    digits(0, NS)
+    order = [(q + d) % N for d in range(N)]
+    for r in order[1:]:
+        onehot(r)
+    for r in order:
         g.tensor.wait_ge(T.sem["oh%d" % r], 2 * DW)
         for c in range(r * DW, r * DW + DW):
-            last = c == NS - 1
-            ins = g.tensor.matmul(T.p1[:], T.A1[:, 128 * c:128 * c + 128], T.B1[:, 32 * c:32 * c + 32], c == 0, last)
+            last = c == order[-1] * DW + DW - 1
+            ins = g.tensor.matmul(T.p1[:], T.A1[:, 128 * c:128 * c + 128], T.B1[:, 32 * c:32 * c + 32], c == q * DW, last)
             if last:
                 ins.then_inc(T.sem.mm, 1)
+    V.wait_ge(T.sem.gi, 7)
     for kh in range(8):
         v(V.tensor_scalar(out=T.SL[:, 128 * kh:128 * kh + 128], in0=T.i16[:], scalar1=T.pm[:, kh:kh + 1],
                           scalar2=None, op0=op.is_equal))
@@ -254,8 +273,8 @@ def rank_program(g, core, T, topo):
     V.tensor_copy(T.O3[:], T.t5[:]).then_inc(T.sem.o3, 1)
     land = 0
     for r in range(N):
-        for k in range(K):
-            o2, n2 = engines(helpers(T.cores[r])[CHUNK[k][0]])
+        for size, slot, who, how in CHUNK:
+            o2, n2 = engines(helpers(T.cores[r])[who])
             land += len(n2) if r == q else len(o2)
     for e in (V, g.scalar):
         e.wait_ge(T.sem.o3, 1)
@@ -275,33 +294,32 @@ def rank_program(g, core, T, topo):
     g.wait_ge(T.sem.lo, sent)
 
 
-def helper_program(g, core, T, r, hs, dest, engines, v, vw):
+def helper_program(g, core, T, r, hs, dest, engines, v, vw, cnt):
     op = AluOpType
     V = g.vector
     me = hs[r].index(core)
     off, on = engines(core)
     roff, ron = engines(T.cores[r])
-    chunks = [k for k in range(K) if CHUNK[k][0] == me]
-    sent = 0
-    heard = {A: len(ron), X: len(off), B: len(off)}[me]
-    stile = T.LS[:, TW * r:TW * r + SW]
-    if me in (A, X):
-        g.wait_ge(T.sem.ls, heard)
-        g.remote_dma_fused([RemoteDMATransfer(dst_ids=[dest(hs[r][X if me == A else B])], dma_engine_mask=sum(off),
-                                              remote_sem=T.sem.ls, srcs=[stile], dsts=[stile])], local_sem=T.sem.lo)
-        sent += len(off)
+    both = len(off) + len(on)
+    size, slot, who, how = [c for c in CHUNK if c[2] == me][0]
+    a, w = slot // 16, size // 16
+    part, fwd, sem = {A: (0, B, "ls"), B: (0, Z, "l2"), Z: (HW, X, "ls"), X: (HW, A, "l2")}[me]
+    g.wait_ge(T.sem.ls, len(ron) // 2 if me in (A, Z) else both)
+    tile = T.LS[:, TW * r + part:TW * r + part + HW]
+    g.remote_dma_fused([RemoteDMATransfer(dst_ids=[dest(hs[r][fwd])], dma_engine_mask=sum(off) + sum(on),
+                                          remote_sem=T.sem[sem], srcs=[tile], dsts=[tile])], local_sem=T.sem.lo)
+    sent = both
     g.iota(T.ip[:], [[0, 1]], 0, 1).then_inc(T.sem.gi, 1)
-    g.iota(T.ic[:, 0:OW], [[16, OW]], 0, 0).then_inc(T.sem.gi, 1)
-    if me == X:
-        k = chunks[0]
+    g.iota(T.ic[:, 0:w], [[16, w]], 0, 0).then_inc(T.sem.gi, 1)
+    if me in (X, Z):
         g.wait_ge(T.sem.rl, len(ron))
-        for call in shares(off, CHUNK[k][1]):
+        for call in shares(off, how):
             tr = []
             for d, eng in call:
-                c = (N - 1 + (-d) % N) * S
-                tr.append(RemoteDMATransfer(dst_ids=[dest(hs[(r + d) % N][X])], dma_engine_mask=sum(eng),
-                                            remote_sem=T.sem["h1_%d" % k], srcs=[T.H[:, (d - 1) * S:d * S]],
-                                            dsts=[T.H[:, c:c + S]]))
+                c = (N - 1 + (-d) % N) * size
+                tr.append(RemoteDMATransfer(dst_ids=[dest(hs[(r + d) % N][me])], dma_engine_mask=sum(eng),
+                                            remote_sem=T.sem.h1, srcs=[T.H[:, (d - 1) * size:d * size]],
+                                            dsts=[T.H[:, c:c + size]]))
                 sent += len(eng)
             g.remote_dma_fused(tr, local_sem=T.sem.lo)
     V.wait_ge(T.sem.gi, 2)
@@ -309,42 +327,41 @@ def helper_program(g, core, T, r, hs, dest, engines, v, vw):
     vw()
     v(V.tensor_copy(T.f15[:], T.q15[:]))
     vw()
-    v(V.tensor_scalar(out=T.C[:, 0:OW], in0=T.ic[:, 0:OW], scalar1=T.f15[:], scalar2=None, op0=op.add))
-    V.wait_ge(T.sem.ls, heard)
-    v(V.tensor_scalar(out=T.ti[:], in0=stile, scalar1=12, scalar2=None, op0=op.arith_shift_right))
+    v(V.tensor_scalar(out=T.C[:, 0:w], in0=T.ic[:, 0:w], scalar1=T.f15[:], scalar2=None, op0=op.add))
+    V.wait_ge(T.sem.l2 if me in (A, Z) else T.sem.ls, both)
+    v(V.tensor_scalar(out=T.ti[:, 0:w], in0=T.LS[:, TW * r + a:TW * r + a + w], scalar1=12, scalar2=None,
+                      op0=op.arith_shift_right))
     vw()
-    v(V.tensor_scalar(out=T.tj[:], in0=T.ti[:], scalar1=float(N - r), scalar2=None, op0=op.add))
+    v(V.tensor_scalar(out=T.tj[:, 0:w], in0=T.ti[:, 0:w], scalar1=float(N - r), scalar2=None, op0=op.add))
     vw()
-    v(V.tensor_scalar(out=T.tk[:], in0=T.tj[:], scalar1=N - 1, scalar2=None, op0=op.bitwise_and))
+    v(V.tensor_scalar(out=T.tk[:, 0:w], in0=T.tj[:, 0:w], scalar1=N - 1, scalar2=None, op0=op.bitwise_and))
     vw()
-    v(V.tensor_scalar(out=T.t1[:, 0:SW], in0=T.tk[:], scalar1=float(S), scalar2=None, op0=op.mult))
+    v(V.tensor_scalar(out=T.t1[:, 0:w], in0=T.tk[:, 0:w], scalar1=float(size), scalar2=None, op0=op.mult))
     vw()
-    for k in chunks:
-        v(V.tensor_tensor(T.t2[:, k * OW:k * OW + OW], T.t1[:, k * OW:k * OW + OW], T.C[:, 0:OW], op.add))
+    v(V.tensor_tensor(T.t2[:, 0:w], T.t1[:, 0:w], T.C[:, 0:w], op.add))
     vw()
-    for k in chunks:
-        v(V.tensor_copy(T.O2[:, k * OW:k * OW + OW], T.t2[:, k * OW:k * OW + OW]))
+    v(V.tensor_copy(T.O2[:, 0:w], T.t2[:, 0:w]))
     vw()
-    for n, k in enumerate(chunks):
-        who, how = CHUNK[k]
-        land = sum(len(eng) for call in shares(roff, how) for d, eng in call)
-        if me == X:
-            V.wait_ge(T.sem.rl, len(ron))
-            c = (N - 1) * S
-        else:
-            land += len(ron)
-            c = n * N * S
-        V.wait_ge(T.sem["h1_%d" % k], land)
-        V.tensor_copy(T.M[:, n * S:n * S + S],
-                      T.H[:, c:c + N * S].indirect(T.O2[:, k * OW:k * OW + OW])).then_inc(T.sem["mg%d" % k], 1)
-        g.wait_ge(T.sem["mg%d" % k], 1)
-        far = [c for i, c in enumerate(T.cores) if i != r]
-        here = T.F[:, r * L + k * S:r * L + k * S + S]
-        src = T.M[:, n * S:n * S + S]
-        g.remote_dma_fused([
-            RemoteDMATransfer(dst_ids=[dest(c) for c in far], dma_engine_mask=sum(off), remote_sem=T.sem.f2,
-                              srcs=[src], dsts=[here for c in far]),
-            RemoteDMATransfer(dst_ids=[dest(T.cores[r])], dma_engine_mask=sum(on), remote_sem=T.sem.f2,
-                              srcs=[src], dsts=[here])], local_sem=T.sem.lo)
-        sent += len(off) + len(on)
+    land = sum(len(eng) for call in shares(roff, how) for d, eng in call)
+    if me not in (X, Z):
+        land += len(ron)
+    h = w // 4 * 2
+    win = T.H[:, (N - 1) * size:(2 * N - 1) * size]
+    g.scalar.wait_ge(T.sem.vs, cnt[0])
+    for e in (V, g.scalar):
+        if me in (X, Z):
+            e.wait_ge(T.sem.rl, len(ron))
+        e.wait_ge(T.sem.h1, land)
+    g.scalar.activation(T.M[:, 0:16 * h], win.indirect(T.O2[:, 0:h]), ActivationFunctionType.Copy).then_inc(T.sem.mg, 1)
+    V.tensor_copy(T.M[:, 16 * h:size], win.indirect(T.O2[:, h:w])).then_inc(T.sem.mg, 1)
+    g.wait_ge(T.sem.mg, 2)
+    far = [T.cores[(r + d) % N] for d in range(1, N)]
+    here = T.F[:, r * L + slot:r * L + slot + size]
+    src = T.M[:, 0:size]
+    g.remote_dma_fused([
+        RemoteDMATransfer(dst_ids=[dest(c) for c in far], dma_engine_mask=sum(off), remote_sem=T.sem.f2,
+                          srcs=[src], dsts=[here for c in far]),
+        RemoteDMATransfer(dst_ids=[dest(T.cores[r])], dma_engine_mask=sum(on), remote_sem=T.sem.f2,
+                          srcs=[src], dsts=[here])], local_sem=T.sem.lo)
+    sent += both
     g.wait_ge(T.sem.lo, sent)

from concourse.bass import DstId, RemoteDMATransfer
from concourse.mybir import AluOpType, ActivationFunctionType

N, R, L = 4, 4096, 1024
A, B, X, Z = 0, 1, 2, 3
CHUNK = [(352, 0, B, "lo"), (160, 512, X, "two"), (160, 352, Z, "two"), (352, 672, A, "hi")]
K = len(CHUNK)
SMAX = max(c[0] for c in CHUNK)
SW, DW = L // 16, L // 128
TW = SW + DW
HW = SW // 2
NS = N * DW
TB = [2048, 1024, 1024]
YB = [256, 256, 512, 512, 768, 768, 512, 512]
KW = R // 16

SCRATCH = {
    "F": ("sbuf", [128, N * L + R], "float32"),
    "G": ("sbuf", [128, N * L], "float32"),
    "Y": ("sbuf", [128, R], "float32"),
    "H": ("sbuf", [128, (2 * N - 1) * SMAX], "float32"),
    "M": ("sbuf", [128, SMAX], "float32"),
    "LS": ("sbuf", [128, N * TW], "int32"),
    "O1": ("sbuf", [128, N * SW], "uint16"),
    "O2": ("sbuf", [128, SW], "uint16"),
    "O3": ("sbuf", [128, KW], "uint16"),
    "DQ": ("sbuf", [128, NS], "int32"),
    "I9": ("sbuf", [128, NS], "int32"),
    "I4": ("sbuf", [128, NS], "int32"),
    "I0": ("sbuf", [128, NS], "int32"),
    "F9": ("sbuf", [128, NS], "float32"),
    "F0": ("sbuf", [128, NS], "float32"),
    "KL": ("sbuf", [128, NS], "float32"),
    "MD": ("sbuf", [128, NS], "float32"),
    "W": ("sbuf", [128, NS], "float32"),
    "iw": ("sbuf", [128, NS], "int32"),
    "ip": ("sbuf", [128, 1], "int32"),
    "pm": ("sbuf", [128, 8], "float32"),
    "q15": ("sbuf", [128, 1], "int32"),
    "q7": ("sbuf", [128, 1], "int32"),
    "q3": ("sbuf", [128, 1], "int32"),
    "f15": ("sbuf", [128, 1], "float32"),
    "f7": ("sbuf", [128, 1], "float32"),
    "f3": ("sbuf", [128, 1], "float32"),
    "ia": ("sbuf", [128, 128], "bfloat16"),
    "i16": ("sbuf", [128, 128], "bfloat16"),
    "ic": ("sbuf", [128, KW], "int32"),
    "C": ("sbuf", [128, KW], "float32"),
    "A1": ("sbuf", [128, NS * 128], "float16"),
    "B1": ("sbuf", [128, NS * 32], "float16"),
    "SL": ("sbuf", [128, 8 * 128], "float16"),
    "X1": ("sbuf", [128, 32], "float16"),
    "t1": ("sbuf", [128, KW], "float32"),
    "t2": ("sbuf", [128, KW], "float32"),
    "t3": ("sbuf", [128, KW], "float32"),
    "t4": ("sbuf", [128, KW], "float32"),
    "t5": ("sbuf", [128, KW], "float32"),
    "ti": ("sbuf", [128, SW], "int32"),
    "tj": ("sbuf", [128, SW], "int32"),
    "tk": ("sbuf", [128, SW], "int32"),
    "p1": ("psum", [128, 32], "float32"),
    "p2": ("psum", [128, KW], "float32"),
}
SEMAPHORES = (["ld", "gate", "tl", "ls", "l2", "o1", "lo", "f2", "gi", "vs", "mm", "m2", "o3", "st", "rl", "h1", "mg"]
              + ["ga%d" % k for k in range(K)] + ["oh%d" % r for r in range(N)] + ["fy%d" % j for j in range(len(YB))])


def bits(m):
    return [1 << e for e in range(16) if (m >> e) & 1]


def shares(off, how):
    n = len(off)
    if how == "lo":
        return [[(1, off[:n // 2]), (2, off[n // 2:3 * n // 4]), (3, off[3 * n // 4:])]]
    if how == "hi":
        return [[(1, off[:n // 4]), (2, off[n // 4:n // 2]), (3, off[n // 2:])]]
    return [[(1, off[:n // 2]), (2, off[n // 2:])], [(3, off)]]


def rank_program(g, core, T, topo):
    op = AluOpType
    V = g.vector

    def helpers(rc):
        c = [x for x in range(256) if topo.host(x) == topo.host(rc) and topo.chip(x) == topo.chip(rc) and x != rc]
        near = [x for x in c if topo.die(x) == topo.die(rc)]
        far = [x for x in c if topo.die(x) != topo.die(rc)]
        return [near[0], far[0], far[1], far[2]]

    def dest(dst):
        rid, pid = topo.addr(dst, core)
        return DstId(rid=rid, pnc=pid)

    def engines(src):
        r = [i for i, c in enumerate(T.cores) if topo.host(c) == topo.host(src) and topo.chip(c) == topo.chip(src)][0]
        near = [c for c in helpers(T.cores[r]) if c != src][0]
        off = topo.mask(src, T.cores[(r + 1) % N])
        return bits(off), bits(topo.mask(src, near) & ~off)

    cnt = [0]

    def v(ins):
        ins.then_inc(T.sem.vs, 1)
        cnt[0] += 1

    def vw():
        V.wait_ge(T.sem.vs, cnt[0])

    q = T.rank_of(core)
    if q is None:
        own = [r for r in range(N) if core in helpers(T.cores[r])]
        if own:
            hs = [helpers(c) for c in T.cores]
            helper_program(g, core, T, own[0], hs, dest, engines, v, vw, cnt)
        return

    off, on = engines(core)
    others = [T.cores[(q + d) % N] for d in range(1, N)]
    mine = helpers(core)
    b = TW * q
    for a in range(8):
        e = g.sync if a % 2 == 0 else g.scalar
        e.dma_start(T.LS[16 * a:16 * a + 16, b:b + SW], T.src[:]).then_inc(T.sem.ld, 16)
    g.scalar.dma_start(T.LS[:, b + SW:b + TW], T.dst[:]).then_inc(T.sem.ld, 16)
    a = 0
    for j, w in enumerate(TB):
        if j == 1:
            g.sync.wait_ge(T.sem.ld, 144)
        if j == 2:
            g.sync.wait_ge(T.sem.gate, 1)
        g.sync.dma_start(T.F[:, N * L + a:N * L + a + w], T.tab[:, a:a + w]).then_inc(T.sem.tl, 16)
        a += w
    g.iota(T.ip[:], [[0, 1]], 0, 1).then_inc(T.sem.gi, 1)
    hw = NS // 2
    g.iota(T.iw[:, 0:hw], [[L, N // 2], [16, DW]], -2048, 0).then_inc(T.sem.gi, 1)
    g.iota(T.iw[:, hw:2 * hw], [[L, N // 2], [16, DW]], 1, 0).then_inc(T.sem.gi, 1)
    g.iota(T.ia[:], [[1, 128]], 0, 0, allow_small_or_imprecise_dtypes=True).then_inc(T.sem.gi, 1)
    tile = T.LS[:, b:b + TW]
    g.wait_ge(T.sem.ld, 144)
    g.remote_dma_fused([RemoteDMATransfer(dst_ids=[dest(c) for c in others], dma_engine_mask=sum(off),
                                          remote_sem=T.sem.ls, srcs=[tile], dsts=[tile for c in others])],
                       local_sem=T.sem.lo)
    g.sem_inc(T.sem.gate, 1)
    h = len(on) // 2
    g.remote_dma_fused([RemoteDMATransfer(dst_ids=[dest(mine[who])], dma_engine_mask=sum(eng), remote_sem=T.sem.ls,
                                          srcs=[T.LS[:, c:c + HW]], dsts=[T.LS[:, c:c + HW]])
                        for who, eng, c in ((A, on[:h], b), (Z, on[h:], b + HW))], local_sem=T.sem.lo)
    sent = len(off) + len(on)
    g.iota(T.pm[:], [[-16, 8]], 0, 1, allow_small_or_imprecise_dtypes=True).then_inc(T.sem.gi, 1)
    g.iota(T.i16[:], [[0, 8], [1, 16]], 0, 0, allow_small_or_imprecise_dtypes=True).then_inc(T.sem.gi, 1)
    g.iota(T.ic[:], [[16, KW]], 0, 0).then_inc(T.sem.gi, 1)

    def offsets(r):
        V.tensor_scalar(out=T.O1[:, SW * r:SW * r + SW], in0=T.LS[:, TW * r:TW * r + SW], scalar1=float(R * q),
                        scalar2=float(R - 1), op0=op.subtract, op1=op.min).then_inc(T.sem.o1, 1)

    def digits(c, n):
        z = slice(c, c + n)
        for r in range(c // DW, (c + n) // DW):
            v(V.tensor_scalar(out=T.DQ[:, DW * r:DW * r + DW], in0=T.LS[:, TW * r + SW:TW * r + TW],
                              scalar1=float(R * q), scalar2=None, op0=op.subtract))
        vw()
        v(V.tensor_scalar(out=T.I9[:, z], in0=T.DQ[:, z], scalar1=9, scalar2=None, op0=op.arith_shift_right))
        v(V.tensor_scalar(out=T.I0[:, z], in0=T.DQ[:, z], scalar1=15, scalar2=None, op0=op.bitwise_and))
        v(V.tensor_scalar(out=T.I4[:, z], in0=T.DQ[:, z], scalar1=4, scalar2=31, op0=op.arith_shift_right,
                          op1=op.bitwise_and))
        vw()
        v(V.tensor_scalar(out=T.F9[:, z], in0=T.I9[:, z], scalar1=16.0, scalar2=None, op0=op.mult))
        v(V.tensor_copy(T.F0[:, z], T.I0[:, z]))
        v(V.tensor_copy(T.KL[:, z], T.I4[:, z]))
        vw()
        v(V.tensor_tensor(T.MD[:, z], T.F9[:, z], T.F0[:, z], op.add))
        vw()

    def onehot(r):
        s = T.sem["oh%d" % r]
        for c in range(r * DW, r * DW + DW):
            V.tensor_scalar(out=T.A1[:, 128 * c:128 * c + 128], in0=T.ia[:], scalar1=T.MD[:, c:c + 1],
                            scalar2=T.W[:, c:c + 1], op0=op.is_equal, op1=op.mult).then_inc(s, 1)
            V.tensor_scalar(out=T.B1[:, 32 * c:32 * c + 32], in0=T.ia[:, 0:32], scalar1=T.KL[:, c:c + 1],
                            scalar2=None, op0=op.is_equal).then_inc(s, 1)

    V.wait_ge(T.sem.ld, 144)
    offsets(q)
    V.wait_ge(T.sem.gi, 4)
    v(V.tensor_scalar(out=T.q15[:], in0=T.ip[:], scalar1=15, scalar2=None, op0=op.bitwise_and))
    v(V.tensor_scalar(out=T.q7[:], in0=T.ip[:], scalar1=7, scalar2=None, op0=op.bitwise_and))
    v(V.tensor_scalar(out=T.q3[:], in0=T.ip[:], scalar1=3, scalar2=None, op0=op.arith_shift_right))
    vw()
    v(V.tensor_copy(T.f15[:], T.q15[:]))
    v(V.tensor_scalar(out=T.f7[:], in0=T.q7[:], scalar1=128.0, scalar2=None, op0=op.mult))
    v(V.tensor_copy(T.f3[:], T.q3[:]))
    vw()
    v(V.tensor_scalar(out=T.W[:], in0=T.iw[:], scalar1=T.f7[:], scalar2=T.f3[:], op0=op.add, op1=op.add))
    digits(q * DW, DW)
    onehot(q)
    V.wait_ge(T.sem.ls, (N - 1) * len(off))
    for r in range(N):
        if r != q:
            offsets(r)
    V.wait_ge(T.sem.o1, N)
    V.wait_ge(T.sem.tl, 16 * len(TB))
    g.scalar.wait_ge(T.sem.o1, N)
    g.scalar.wait_ge(T.sem.tl, 16 * len(TB))
    win = T.F[:, N * L:N * L + R]

    def cand(k, d):
        size, slot = CHUNK[k][:2]
        c = N * slot + (d - 1) % N * size
        return T.G[:, c:c + size]
    for k in range(K):
        size, slot = CHUNK[k][:2]
        for d in range(N):
            c = SW * ((q + d) % N) + slot // 16
            idx = T.O1[:, c:c + size // 16]
            if d < N // 2:
                V.tensor_copy(cand(k, d), win.indirect(idx)).then_inc(T.sem["ga%d" % k], 1)
            else:
                g.scalar.activation(cand(k, d), win.indirect(idx),
                                    ActivationFunctionType.Copy).then_inc(T.sem["ga%d" % k], 1)
    for k in range(K):
        size, slot, who, how = CHUNK[k]
        g.wait_ge(T.sem["ga%d" % k], N)
        if who in (X, Z):
            g.remote_dma_fused([RemoteDMATransfer(dst_ids=[dest(mine[who])], dma_engine_mask=sum(on),
                                                  remote_sem=T.sem.rl, srcs=[T.G[:, N * slot:N * (slot + size)]],
                                                  dsts=[T.H[:, 0:N * size]])], local_sem=T.sem.lo)
            sent += len(on)
            continue
        for i, call in enumerate(shares(off, how)):
            tr = []
            for d, eng in call + ([(0, on)] if i == 0 else []):
                hc = helpers(T.cores[(q + d) % N])[who]
                c = (N - 1 + (-d) % N) * size
                tr.append(RemoteDMATransfer(dst_ids=[dest(hc)], dma_engine_mask=sum(eng), remote_sem=T.sem.h1,
                                            srcs=[cand(k, d)], dsts=[T.H[:, c:c + size]]))
                sent += len(eng)
            g.remote_dma_fused(tr, local_sem=T.sem.lo)

    digits(0, NS)
    order = [(q + d) % N for d in range(N)]
    for r in order[1:]:
        onehot(r)
    for r in order:
        g.tensor.wait_ge(T.sem["oh%d" % r], 2 * DW)
        for c in range(r * DW, r * DW + DW):
            last = c == order[-1] * DW + DW - 1
            ins = g.tensor.matmul(T.p1[:], T.A1[:, 128 * c:128 * c + 128], T.B1[:, 32 * c:32 * c + 32], c == q * DW, last)
            if last:
                ins.then_inc(T.sem.mm, 1)
    V.wait_ge(T.sem.gi, 7)
    for kh in range(8):
        v(V.tensor_scalar(out=T.SL[:, 128 * kh:128 * kh + 128], in0=T.i16[:], scalar1=T.pm[:, kh:kh + 1],
                          scalar2=None, op0=op.is_equal))
    v(V.tensor_scalar(out=T.C[:], in0=T.ic[:], scalar1=T.f15[:], scalar2=float(N * L - 2048), op0=op.add, op1=op.add))
    V.wait_ge(T.sem.mm, 1)
    v(V.tensor_copy(T.X1[:], T.p1[:]))
    g.tensor.wait_ge(T.sem.vs, cnt[0])
    for kh in range(8):
        g.tensor.matmul(T.p2[:, 32 * kh:32 * kh + 32], T.SL[:, 128 * kh:128 * kh + 128], T.X1[:], True,
                        True).then_inc(T.sem.m2, 1)
    vw()
    V.wait_ge(T.sem.m2, 8)
    v(V.tensor_scalar(out=T.t1[:], in0=T.p2[:], scalar1=0.0, scalar2=None, op0=op.is_equal))
    v(V.tensor_scalar(out=T.t2[:], in0=T.p2[:], scalar1=0.0, scalar2=2047.0, op0=op.is_le, op1=op.add))
    vw()
    v(V.tensor_tensor(T.t3[:], T.t1[:], T.C[:], op.mult))
    v(V.tensor_tensor(T.t4[:], T.t2[:], T.p2[:], op.add))
    vw()
    v(V.tensor_tensor(T.t5[:], T.t3[:], T.t4[:], op.add))
    vw()
    V.tensor_copy(T.O3[:], T.t5[:]).then_inc(T.sem.o3, 1)
    land = 0
    for r in range(N):
        for size, slot, who, how in CHUNK:
            o2, n2 = engines(helpers(T.cores[r])[who])
            land += len(n2) if r == q else len(o2)
    for e in (V, g.scalar):
        e.wait_ge(T.sem.o3, 1)
        e.wait_ge(T.sem.f2, land)
    c = 0
    for j, w in enumerate(YB):
        src = T.F[:].indirect(T.O3[:, c // 16:(c + w) // 16])
        s = T.sem["fy%d" % j]
        if j % 2 == 0:
            V.tensor_copy(T.Y[:, c:c + w], src).then_inc(s, 1)
        else:
            g.scalar.activation(T.Y[:, c:c + w], src, ActivationFunctionType.Copy).then_inc(s, 1)
        g.sync.wait_ge(s, 1)
        g.sync.dma_start(T.y[:, c:c + w], T.Y[:, c:c + w]).then_inc(T.sem.st, 16)
        c += w
    g.sync.wait_ge(T.sem.st, 16 * len(YB))
    g.wait_ge(T.sem.lo, sent)


def helper_program(g, core, T, r, hs, dest, engines, v, vw, cnt):
    op = AluOpType
    V = g.vector
    me = hs[r].index(core)
    off, on = engines(core)
    roff, ron = engines(T.cores[r])
    both = len(off) + len(on)
    size, slot, who, how = [c for c in CHUNK if c[2] == me][0]
    a, w = slot // 16, size // 16
    part, fwd, sem = {A: (0, B, "ls"), B: (0, Z, "l2"), Z: (HW, X, "ls"), X: (HW, A, "l2")}[me]
    g.wait_ge(T.sem.ls, len(ron) // 2 if me in (A, Z) else both)
    tile = T.LS[:, TW * r + part:TW * r + part + HW]
    g.remote_dma_fused([RemoteDMATransfer(dst_ids=[dest(hs[r][fwd])], dma_engine_mask=sum(off) + sum(on),
                                          remote_sem=T.sem[sem], srcs=[tile], dsts=[tile])], local_sem=T.sem.lo)
    sent = both
    g.iota(T.ip[:], [[0, 1]], 0, 1).then_inc(T.sem.gi, 1)
    g.iota(T.ic[:, 0:w], [[16, w]], 0, 0).then_inc(T.sem.gi, 1)
    if me in (X, Z):
        g.wait_ge(T.sem.rl, len(ron))
        for call in shares(off, how):
            tr = []
            for d, eng in call:
                c = (N - 1 + (-d) % N) * size
                tr.append(RemoteDMATransfer(dst_ids=[dest(hs[(r + d) % N][me])], dma_engine_mask=sum(eng),
                                            remote_sem=T.sem.h1, srcs=[T.H[:, (d - 1) * size:d * size]],
                                            dsts=[T.H[:, c:c + size]]))
                sent += len(eng)
            g.remote_dma_fused(tr, local_sem=T.sem.lo)
    V.wait_ge(T.sem.gi, 2)
    v(V.tensor_scalar(out=T.q15[:], in0=T.ip[:], scalar1=15, scalar2=None, op0=op.bitwise_and))
    vw()
    v(V.tensor_copy(T.f15[:], T.q15[:]))
    vw()
    v(V.tensor_scalar(out=T.C[:, 0:w], in0=T.ic[:, 0:w], scalar1=T.f15[:], scalar2=None, op0=op.add))
    V.wait_ge(T.sem.l2 if me in (A, Z) else T.sem.ls, both)
    v(V.tensor_scalar(out=T.ti[:, 0:w], in0=T.LS[:, TW * r + a:TW * r + a + w], scalar1=12, scalar2=None,
                      op0=op.arith_shift_right))
    vw()
    v(V.tensor_scalar(out=T.tj[:, 0:w], in0=T.ti[:, 0:w], scalar1=float(N - r), scalar2=None, op0=op.add))
    vw()
    v(V.tensor_scalar(out=T.tk[:, 0:w], in0=T.tj[:, 0:w], scalar1=N - 1, scalar2=None, op0=op.bitwise_and))
    vw()
    v(V.tensor_scalar(out=T.t1[:, 0:w], in0=T.tk[:, 0:w], scalar1=float(size), scalar2=None, op0=op.mult))
    vw()
    v(V.tensor_tensor(T.t2[:, 0:w], T.t1[:, 0:w], T.C[:, 0:w], op.add))
    vw()
    v(V.tensor_copy(T.O2[:, 0:w], T.t2[:, 0:w]))
    vw()
    land = sum(len(eng) for call in shares(roff, how) for d, eng in call)
    if me not in (X, Z):
        land += len(ron)
    h = w // 4 * 2
    win = T.H[:, (N - 1) * size:(2 * N - 1) * size]
    g.scalar.wait_ge(T.sem.vs, cnt[0])
    for e in (V, g.scalar):
        if me in (X, Z):
            e.wait_ge(T.sem.rl, len(ron))
        e.wait_ge(T.sem.h1, land)
    g.scalar.activation(T.M[:, 0:16 * h], win.indirect(T.O2[:, 0:h]), ActivationFunctionType.Copy).then_inc(T.sem.mg, 1)
    V.tensor_copy(T.M[:, 16 * h:size], win.indirect(T.O2[:, h:w])).then_inc(T.sem.mg, 1)
    g.wait_ge(T.sem.mg, 2)
    far = [T.cores[(r + d) % N] for d in range(1, N)]
    here = T.F[:, r * L + slot:r * L + slot + size]
    src = T.M[:, 0:size]
    g.remote_dma_fused([
        RemoteDMATransfer(dst_ids=[dest(c) for c in far], dma_engine_mask=sum(off), remote_sem=T.sem.f2,
                          srcs=[src], dsts=[here for c in far]),
        RemoteDMATransfer(dst_ids=[dest(T.cores[r])], dma_engine_mask=sum(on), remote_sem=T.sem.f2,
                          srcs=[src], dsts=[here])], local_sem=T.sem.lo)
    sent += both
    g.wait_ge(T.sem.lo, sent)
